import numpy as np
import ml_dtypes


def mxq(x, axis, fmt="e4m3"):
    dtype, down = {"e4m3": (ml_dtypes.float8_e4m3fn, 7), "e5m2": (ml_dtypes.float8_e5m2, 14)}[fmt]
    v = np.moveaxis(np.asarray(x, np.float32).astype(ml_dtypes.bfloat16).astype(np.float64), axis, -1)
    blocks = v.reshape(v.shape[:-1] + (-1, 32))
    amax = np.abs(blocks).max(-1, keepdims=True)
    byte = np.maximum(np.where(amax > 0, np.frexp(amax)[1] - 1 + 127, 0) - down, 1)
    scale = np.exp2(byte - 127.0)
    codes = (blocks / scale).astype(np.float32).astype(dtype).astype(np.float64)
    return np.moveaxis((codes * scale).reshape(v.shape), -1, axis)


WIDE = False


def mx_kscale(k):
    if not WIDE:
        return np.ones(k)
    levels = np.array([10, -10, 5, -5, 0])
    if k % 512:
        return np.exp2(np.random.permutation(np.resize(levels, k // 32))).repeat(32)
    a = np.empty((k // 512, 16))
    for p in range(k // 512):
        a[p, :8] = np.random.permutation(np.resize(levels, 8))
        for g in range(8):
            far = levels[np.abs(levels - a[p, g]) >= 10]
            a[p, g + 8] = far[np.random.randint(len(far))]
    return np.exp2(a.ravel()).repeat(32)


def f64(x):
    return np.asarray(x).astype(np.float64)


def striped(idx):
    return np.tile(idx.reshape(-1, 16).T, (8, 1)).astype(np.uint16)


def unstriped(offs):
    return offs[:16].T.reshape(-1).astype(np.int64)


def striped8(idx):
    return np.concatenate([x.reshape(-1, 16).T for x in idx]).astype(np.uint16)


def runs(offs, k):
    lists = np.stack([offs[16 * r : 16 * r + 16].T.reshape(-1) for r in range(8)]).astype(np.int64)
    return lists[np.arange(k) % 512 // 64]


def pack_weight(w):
    k, n = w.shape
    w = f64(np.asarray(w, np.float32).astype(ml_dtypes.bfloat16)).reshape(k // 32, 32, n)
    amax = np.abs(w).max(1)
    byte = np.clip(np.where(amax > 0, np.frexp(amax)[1] - 1 + 127 - 7, 1), 1, 254)
    scaled = (w * np.exp2(127.0 - byte)[:, None, :]).reshape(k, n).astype(np.float32)
    words = np.ascontiguousarray(scaled.reshape(k // 512, 128, 4, n).transpose(0, 1, 3, 2)).astype(ml_dtypes.float8_e4m3fn).view(np.uint8)
    return words, np.ascontiguousarray(byte.astype(np.uint8).reshape(k // 512, 16, n))


def unpack_weight(words, scales):
    g, p, n, _ = words.shape
    vals = np.ascontiguousarray(words).view(ml_dtypes.float8_e4m3fn).astype(np.float64) * np.repeat(np.exp2(scales.astype(np.float64) - 127.0), 8, axis=1)[..., None]
    return vals.transpose(0, 1, 3, 2).reshape(g * 512, n)


def sigmoid(v):
    return 1.0 / (1.0 + np.exp(-np.maximum(v, -700.0)))

def planes(y):
    n, m = y.shape
    v = y.astype(np.float32).astype(ml_dtypes.bfloat16).astype(np.float64).reshape(n // 32, 32, m)
    top = np.abs(v).max(1)
    byte = np.clip(np.where(top > 0, np.frexp(top)[1] - 1 + 127 - 7, 1), 1, 254)
    codes = (v * np.exp2(127.0 - byte)[:, None, :]).reshape(n, m).astype(np.float32).astype(ml_dtypes.float8_e4m3fn).view(np.uint8)
    words = codes.reshape(n // 512, 128, 4, m).transpose(0, 1, 3, 2)
    return np.ascontiguousarray(words), np.ascontiguousarray(byte.astype(np.uint8).reshape(n // 512, 16, m))


K, T, S, N, H = 512, 2048, 512, 512, 512


def setup_inputs():
    n = np.random.standard_normal
    s = mx_kscale(K)[:, None]
    u = mx_kscale(S)
    packed_xT = pack_weight(n((K, T)) * s)
    packed_w1 = pack_weight(n((S, N)) / np.sqrt(S) / u[:, None])
    return {
        "x_words": packed_xT[0],
        "x_scales": packed_xT[1],
        "wa": (n((K, H)) / np.sqrt(K) / s).astype(np.float32),
        "wb": (n((K, H)) / np.sqrt(K) / s).astype(np.float32),
        "sl": np.random.uniform(1.0, 2.0, (S, 1)).astype(np.float32),
        "th": (0.5 * n((S, 1))).astype(np.float32),
        "gt": (np.random.uniform(0.5, 1.5, (S, 1)) * u[:, None]).astype(np.float32),
        "w1_words": packed_w1[0],
        "w1_scales": packed_w1[1],
        "offs": striped(np.random.permutation(T)[:S]),
        "two": striped(np.random.permutation(T)[:S]),
        "n1": striped(np.random.permutation(H)),
        "n2": striped(np.random.permutation(H)),
        "n3": striped8(np.stack([np.random.permutation(H) for _ in range(8)])),
        "n4": striped8(np.stack([np.random.permutation(H) for _ in range(8)])),
    }


def reference(x_words, x_scales, wa, wb, sl, th, gt, w1_words, w1_scales, offs, two, n1, n2, n3, n4):
    xq = unpack_weight(x_words, x_scales)[:, unstriped(offs)]
    y = xq.T @ mxq(f64(wa), 0, "e4m3")
    x_two = unpack_weight(x_words, x_scales)[:, unstriped(two)]
    d = x_two.T @ mxq(f64(wb), 0, "e4m3")
    sg = sigmoid(f64(sl) * (d[:, unstriped(n1)] - f64(th)))
    z = f64(gt) * (y * sg - (0.5 * y[:, unstriped(n2)]))
    h = unpack_weight(w1_words, w1_scales).T @ mxq(z, 0, "e4m3")
    ex = np.exp(h)
    out_0 = np.log(ex + ex[np.arange(N)[:, None], runs(n3, N)]) - (h[np.arange(N)[:, None], runs(n4, N)])
    return (out_0,) + planes(out_0)

@@ -1,0 +1,257 @@
+from contextlib import ExitStack
+
+import concourse.mybir as mybir
+
+K, T, S, N, H = 512, 2048, 512, 512, 512
+FLOPS = 3 * 2 * 512 * 512 * 512
+
+F32 = mybir.dt.float32
+BF16 = mybir.dt.bfloat16
+I32 = mybir.dt.int32
+U32 = mybir.dt.uint32
+U16 = mybir.dt.uint16
+U8 = mybir.dt.uint8
+FP8X4 = mybir.dt.float8_e4m3fn_x4
+ALU = mybir.AluOpType
+ACT = mybir.ActivationFunctionType
+
+P = 128
+PACK = 4
+HALF = 256
+LIST_ROWS = 16
+
+
+def tile_picked_twtgxblse_none_po_kernel(
+    tc, x_words, x_scales, wa, wb, sl, th, gt, w1_words, w1_scales, offs, two, n1, n2, n3, n4, out_0, out_1, out_2
+):
+    nc = tc.nc
+    halves = [slice(u * HALF, (u + 1) * HALF) for u in range(2)]
+
+    with ExitStack() as ctx:
+        keep = ctx.enter_context(tc.tile_pool(name="keep", bufs=1))
+        psum = ctx.enter_context(tc.psum_pool(name="psum", bufs=1))
+
+        def load_list(name, source):
+            tile = keep.tile([P, 512 // LIST_ROWS], U16, name=name)
+            nc.sync.dma_start(tile[:], source)
+            return tile
+
+        def entries(tile, cols):
+            return tile[:, cols.start // LIST_ROWS : cols.stop // LIST_ROWS]
+
+        def load_scale_rows(queue, tile, source):
+            for q in range(4):
+                queue.dma_start(tile[32 * q : 32 * q + 4, :].bitcast(I32), source[0, 4 * q : 4 * q + 4, :].bitcast(I32))
+
+        def load_words(tile, source):
+            nc.sync.dma_start(tile[:].bitcast(I32), source[0].rearrange("p c t -> p (c t)").bitcast(I32))
+
+        def load_weight_half(name, w, cols):
+            raw = keep.tile([P, PACK, HALF], F32, name=name, align_bytes=64)
+            nc.sync.dma_start(raw[:], w.rearrange("(p j) c -> p j c", j=PACK)[:, :, cols])
+            return raw
+
+        def load_rows(name, source):
+            tile = keep.tile([P, PACK], F32, name=name)
+            nc.scalar.dma_start(tile[:], source.rearrange("(p t) o -> p (t o)", t=PACK))
+            return tile
+
+        def interleave(copy, name, planes):
+            grouped = keep.tile([P, planes.shape[2], PACK], BF16, name=name, align_bytes=64)
+            copy(
+                grouped[:].rearrange("p (c i) t -> p c t i", i=4),
+                planes.rearrange("p t (c i) -> p c t i", i=4),
+            )
+            return grouped
+
+        def quantise(codes, scales, cols, grouped):
+            nc.vector.quantize_mx(
+                out=codes[:, cols].bitcast(FP8X4), scales=scales[:, cols], in_=grouped[:].rearrange("p c t -> p (c t)")
+            )
+
+        def mx_tiles(name, width, codes_tag="", scales_tag=""):
+            codes = keep.tile([P, width], U32, name=name + "_codes", tag=codes_tag, align_bytes=64)
+            scales = keep.tile([P, width], U8, name=name + "_scales", tag=scales_tag, align_bytes=64)
+            return codes, scales
+
+        def dealt(ap):
+            return ap.rearrange("p (t m) -> p m t", t=PACK)
+
+        def product(target, cols, lhs, t, rhs):
+            rows = slice(P * t, P * (t + 1))
+            nc.tensor.matmul_mx(
+                out=target,
+                lhsT=lhs[0][:, rows].bitcast(FP8X4),
+                lhsT_scale=lhs[1][:, rows],
+                rhs=rhs[0][:, cols].bitcast(FP8X4),
+                rhs_scale=rhs[1][:, cols],
+                start=True,
+                stop=True,
+            )
+
+        def planes(name, tags=("",) * PACK):
+            return [keep.tile([P, H], F32, name="%s%d" % (name, t), tag=tags[t], align_bytes=64) for t in range(PACK)]
+
+        x_codes, x_bytes = mx_tiles("x", T)
+        w1_codes, w1_bytes = mx_tiles("w1", N)
+        nc.vector.memset(x_bytes[:].bitcast(I32), 0)
+        nc.vector.memset(w1_bytes[:].bitcast(I32), 0)
+        two_list = load_list("two_list", two)
+        offs_list = load_list("offs_list", offs)
+        n1_list = load_list("n1_list", n1)
+        slope = load_rows("slope", sl)
+        threshold = load_rows("threshold", th)
+        gate = load_rows("gate", gt)
+        load_words(x_codes, x_words)
+        wb_raw = [load_weight_half("wb_raw0", wb, halves[0])]
+        load_scale_rows(nc.sync, x_bytes, x_scales)
+        n2_list = load_list("n2_list", n2)
+        wb_raw.append(load_weight_half("wb_raw1", wb, halves[1]))
+        wa_raw = [load_weight_half("wa_raw%d" % u, wa, halves[u]) for u in range(2)]
+        load_words(w1_codes, w1_words)
+        load_scale_rows(nc.sync, w1_bytes, w1_scales)
+        n3_list = load_list("n3_list", n3)
+        n4_list = load_list("n4_list", n4)
+
+        slope_threshold = keep.tile([P, PACK], F32, name="slope_threshold")
+        nc.gpsimd.tensor_tensor(slope_threshold[:], threshold[:], slope[:], ALU.mult)
+        bias = keep.tile([P, PACK], F32, name="bias")
+        nc.gpsimd.tensor_scalar(bias[:], slope_threshold[:], -1.0, 0.0, ALU.mult, ALU.add)
+        half_gate = keep.tile([P, PACK], F32, name="half_gate")
+        nc.gpsimd.tensor_scalar(half_gate[:], gate[:], -0.5, 0.0, ALU.mult, ALU.add)
+
+        def pick(gathered, table, picks):
+            nc.vector.tensor_copy(dealt(gathered[:]), table[:].indirect(picks[:]))
+
+        banks = [psum.tile([P, H], F32, name="bank%d" % b) for b in range(2 * PACK)]
+        d_banks, y_banks = banks[:PACK], banks[PACK:]
+        wb_grouped = [interleave(nc.scalar.copy, "wb_grouped%d" % u, wb_raw[u][:]) for u in range(2)]
+        wa_grouped = [interleave(nc.scalar.copy, "wa_grouped%d" % u, wa_raw[u][:]) for u in range(2)]
+        x_two, wb_q, wa_q = mx_tiles("x_two", S), mx_tiles("wb_q", H), mx_tiles("wa_q", H)
+        pick(x_two[0], x_codes, two_list)
+        pick(x_two[1], x_bytes, two_list)
+        quantise(wb_q[0], wb_q[1], halves[0], wb_grouped[0])
+        x_idx_codes = keep.tile([P, S], U32, name="x_idx_codes", tag="", align_bytes=64)
+        pick(x_idx_codes, x_codes, offs_list)
+        quantise(wb_q[0], wb_q[1], halves[1], wb_grouped[1])
+        x_idx_scales = keep.tile([P, S], U8, name="x_idx_scales", tag="wb_grouped1", align_bytes=64)
+        pick(x_idx_scales, x_bytes, offs_list)
+        x_idx = (x_idx_codes, x_idx_scales)
+        for cols in halves:
+            for t in range(PACK):
+                product(d_banks[t][:, cols], cols, x_two, t, wb_q)
+        for u in range(2):
+            quantise(wa_q[0], wa_q[1], halves[u], wa_grouped[u])
+        for t in range(PACK):
+            product(y_banks[t][:], slice(0, H), x_idx, t, wa_q)
+
+        w1_dealt = mx_tiles("w1_dealt", N, "wa_grouped1", "w1_codes")
+        nc.vector.tensor_copy(dealt(w1_dealt[0][:]), w1_codes[:].rearrange("p (m t) -> p m t", t=PACK))
+        nc.vector.tensor_copy(dealt(w1_dealt[1][:]), w1_bytes[:].rearrange("p (m t) -> p m t", t=PACK))
+
+        d_rows = planes("d_rows", ("wa_raw1", "wa_raw0", "wa_grouped0", "wb_grouped1"))
+        y_rows, sg, gated = planes("y_rows"), planes("sg"), planes("gated")
+        z = [keep.tile([P, PACK, HALF], F32, name="z%d" % u) for u in range(2)]
+
+        def gate_values(t, cols):
+            nc.scalar.activation(
+                sg[t][:, cols],
+                d_rows[t][:].indirect(entries(n1_list, cols)),
+                ACT.Sigmoid,
+                bias=bias[:, t : t + 1],
+                scale=slope[:, t : t + 1],
+            )
+
+        def apply_gate(t, u):
+            cols = halves[u]
+            nc.vector.scalar_tensor_tensor(gated[t][:, cols], y_rows[t][:, cols], -2.0, sg[t][:, cols], ALU.mult, ALU.mult)
+
+        def mix(t, u):
+            cols = halves[u]
+            nc.vector.tensor_tensor(z[u][:, t, :], y_rows[t][:].indirect(entries(n2_list, cols)), gated[t][:, cols], ALU.add)
+
+        for t in range(PACK):
+            nc.scalar.copy(d_rows[t][:], d_banks[t][:])
+            if t > 0:
+                gate_values(t - 1, halves[0])
+        gate_values(PACK - 1, halves[0])
+        for t in range(3):
+            nc.vector.tensor_scalar(y_rows[t][:], y_banks[t][:], half_gate[:, t : t + 1], None, ALU.mult)
+        for t in range(3, PACK):
+            nc.scalar.activation(y_rows[t][:], y_banks[t][:], ACT.Copy, scale=half_gate[:, t : t + 1])
+        for t in range(PACK):
+            gate_values(t, halves[1])
+
+        z_q = mx_tiles("z_q", H)
+        h_banks = [[psum.tile([P, HALF], F32, name="bank%d" % (PACK * u + t)) for t in range(PACK)] for u in range(2)]
+        steps = [(t, u) for u in range(2) for t in range(PACK)]
+        for i, (t, u) in enumerate(steps):
+            apply_gate(t, u)
+            if i > 0:
+                mix(*steps[i - 1])
+            if i == 6:
+                quantise(z_q[0], z_q[1], halves[0], interleave(nc.scalar.copy, "z_grouped0", z[0][:]))
+        mix(*steps[-1])
+        quantise(z_q[0], z_q[1], halves[1], interleave(nc.vector.tensor_copy, "z_grouped1", z[1][:]))
+        for u in range(2):
+            for t in range(PACK):
+                product(h_banks[u][t][:], halves[u], w1_dealt, t, z_q)
+
+        ex, ex_again, sums, logs, minus_h = planes("ex"), planes("ex_again"), planes("sums"), planes("logs"), planes("minus_h")
+        for u, cols in enumerate(halves):
+            for t in range(PACK):
+                nc.scalar.activation(ex[t][:, cols], h_banks[u][t][:], ACT.Exp)
+            for t in [1, 2, 3]:
+                nc.scalar.activation(ex_again[t][:, cols], h_banks[u][t][:], ACT.Exp)
+        for u, t in [(0, t) for t in range(PACK)]:
+            nc.vector.tensor_scalar(minus_h[t][:, halves[u]], h_banks[u][t][:], -1.0, None, ALU.mult)
+        copied = [t for t in range(PACK) if t not in [1, 2, 3] and t not in []]
+        for t in copied[:1]:
+            nc.vector.tensor_copy(ex_again[t][:], ex[t][:])
+        for t in []:
+            for cols in halves:
+                nc.scalar.activation(ex_again[t][:, cols], ex[t][:].indirect(entries(n3_list, cols)), ACT.Copy)
+        for t in range(PACK):
+            if t + 1 in copied[1:]:
+                nc.vector.tensor_copy(ex_again[t + 1][:], ex[t + 1][:])
+            if t in []:
+                if t not in []:
+                    for cols in halves:
+                        nc.scalar.activation(ex_again[t][:, cols], ex[t][:].indirect(entries(n3_list, cols)), ACT.Copy)
+                nc.vector.tensor_tensor(sums[t][:], ex[t][:], ex_again[t][:], ALU.add)
+            else:
+                for cols in halves:
+                    nc.vector.tensor_tensor(sums[t][:, cols], ex[t][:].indirect(entries(n3_list, cols)), ex_again[t][:, cols], ALU.add)
+            nc.scalar.activation(logs[t][:], sums[t][:], ACT.Ln)
+            for u, cols in enumerate(halves):
+                if (u, t) not in [(0, t) for t in range(PACK)]:
+                    nc.scalar.activation(minus_h[t][:, cols], h_banks[u][t][:], ACT.Copy, scale=-1.0)
+
+        out_q = mx_tiles("out_q", H)
+        out_rows = out_0.rearrange("(p t) c -> p t c", t=PACK)
+        out_words = out_1[0].rearrange("p c t -> p (c t)").bitcast(I32)
+        chunks = halves
+        fetched = {}
+        for c, cols in enumerate(chunks):
+            for t in range(PACK):
+                if (c, t) in [(1, 1), (1, 2), (1, 3)]:
+                    fetched[c, t] = keep.tile([P, cols.stop - cols.start], F32, name="fetched%d_%d" % (c, t))
+                    nc.scalar.activation(fetched[c, t][:], minus_h[t][:].indirect(entries(n4_list, cols)), ACT.Copy)
+        late = []
+        for c, cols in enumerate(chunks):
+            result = keep.tile([P, PACK, cols.stop - cols.start], F32, name="result%d" % c)
+            for t in range(PACK):
+                if (c, t) in fetched:
+                    nc.vector.tensor_tensor(result[:, t, :], fetched[c, t][:], logs[t][:, cols], ALU.add)
+                else:
+                    nc.vector.tensor_tensor(result[:, t, :], minus_h[t][:].indirect(entries(n4_list, cols)), logs[t][:, cols], ALU.add)
+                if t % 2:
+                    nc.sync.dma_start(out_rows[:, t - 1 : t + 1, cols], result[:, t - 1 : t + 1, :])
+            copy = nc.scalar.copy if c + 1 < len(chunks) else nc.vector.tensor_copy
+            late.append((cols, interleave(copy, "out_grouped%d" % c, result[:])))
+        for cols, grouped in late:
+            quantise(out_q[0], out_q[1], cols, grouped)
+            nc.sync.dma_start(out_words[:, cols], out_q[0][:, cols].bitcast(I32))
+        for q in range(4):
+            queue = nc.scalar if q % 2 else nc.sync
+            queue.dma_start(out_2[0, 4 * q : 4 * q + 4, :].bitcast(I32), out_q[1][32 * q : 32 * q + 4, :].bitcast(I32))

@@ -112,6 +112,9 @@ def tile_picked_twtgxblse_none_po_kernel(
         load_scale_rows(nc.sync, w1_bytes, w1_scales)
         n3_list = load_list("n3_list", n3)
         n4_list = load_list("n4_list", n4)
+        warm = keep.tile([P, 2], F32, name="warm")
+        nc.vector.memset(warm[:, 0:1], 0.0)
+        nc.scalar.activation(warm[:, 1:2], warm[:, 0:1], ACT.Sigmoid)
 
         slope_threshold = keep.tile([P, PACK], F32, name="slope_threshold")
         nc.gpsimd.tensor_tensor(slope_threshold[:], threshold[:], slope[:], ALU.mult)

@@ -123,36 +123,47 @@ def tile_picked_twtgxblse_none_po_kernel(
         half_gate = keep.tile([P, PACK], F32, name="half_gate")
         nc.gpsimd.tensor_scalar(half_gate[:], gate[:], -0.5, 0.0, ALU.mult, ALU.add)
 
-        def pick(gathered, table, picks):
-            nc.vector.tensor_copy(dealt(gathered[:]), table[:].indirect(picks[:]))
+        def deal_words(target, source):
+            nc.vector.tensor_copy(
+                target[:].rearrange("p (t b i) -> p b t i", t=PACK, i=4), source[:].rearrange("p (b i t) -> p b t i", t=PACK, i=4)
+            )
+
+        def deal_bytes(target, source):
+            nc.vector.tensor_copy(target[:].rearrange("p (t m) -> p t m", t=PACK), source[:].rearrange("p (m t) -> p t m", t=PACK))
+
+        def pick_words(target, picks, name):
+            picked = keep.tile([P, S], U32, name=name, align_bytes=64)
+            nc.vector.tensor_copy(picked[:], x_codes[:].indirect(picks[:]))
+            deal_words(target, picked)
+
+        def pick_bytes(target, picks, name, tag=""):
+            picked = keep.tile([P, S], U8, name=name, tag=tag, align_bytes=64)
+            nc.vector.tensor_copy(picked[:], x_bytes[:].indirect(picks[:]))
+            deal_bytes(target, picked)
 
         banks = [psum.tile([P, H], F32, name="bank%d" % b) for b in range(2 * PACK)]
         d_banks, y_banks = banks[:PACK], banks[PACK:]
         wb_grouped = [interleave(nc.scalar.copy, "wb_grouped%d" % u, wb_raw[u][:]) for u in range(2)]
         wa_grouped = [interleave(nc.scalar.copy, "wa_grouped%d" % u, wa_raw[u][:]) for u in range(2)]
-        x_two, wb_q, wa_q = mx_tiles("x_two", S), mx_tiles("wb_q", H), mx_tiles("wa_q", H)
-        pick(x_two[0], x_codes, two_list)
-        pick(x_two[1], x_bytes, two_list)
-        quantise(wb_q[0], wb_q[1], halves[0], wb_grouped[0])
-        x_idx_codes = keep.tile([P, S], U32, name="x_idx_codes", tag="", align_bytes=64)
-        pick(x_idx_codes, x_codes, offs_list)
-        quantise(wb_q[0], wb_q[1], halves[1], wb_grouped[1])
-        x_idx_scales = keep.tile([P, S], U8, name="x_idx_scales", tag="wb_grouped1", align_bytes=64)
-        pick(x_idx_scales, x_bytes, offs_list)
-        x_idx = (x_idx_codes, x_idx_scales)
-        for cols in halves:
-            for t in range(PACK):
-                product(d_banks[t][:, cols], cols, x_two, t, wb_q)
+        x_two, x_idx, wb_q, wa_q = mx_tiles("x_two", S), mx_tiles("x_idx", S), mx_tiles("wb_q", H), mx_tiles("wa_q", H)
+        pick_words(x_two[0], two_list, "two_words")
+        pick_words(x_idx[0], offs_list, "offs_words")
+        pick_bytes(x_two[1], two_list, "two_bytes")
+        for u in range(2):
+            quantise(wb_q[0], wb_q[1], halves[u], wb_grouped[u])
+        pick_bytes(x_idx[1], offs_list, "offs_bytes", "wb_grouped1")
+        for t in range(PACK):
+            product(d_banks[t][:], slice(0, H), x_two, t, wb_q)
         for u in range(2):
             quantise(wa_q[0], wa_q[1], halves[u], wa_grouped[u])
         for t in range(PACK):
             product(y_banks[t][:], slice(0, H), x_idx, t, wa_q)
 
         w1_dealt = mx_tiles("w1_dealt", N, "wa_grouped1", "w1_codes")
-        nc.vector.tensor_copy(dealt(w1_dealt[0][:]), w1_codes[:].rearrange("p (m t) -> p m t", t=PACK))
-        nc.vector.tensor_copy(dealt(w1_dealt[1][:]), w1_bytes[:].rearrange("p (m t) -> p m t", t=PACK))
+        deal_words(w1_dealt[0], w1_codes)
+        deal_bytes(w1_dealt[1], w1_bytes)
 
-        d_rows = planes("d_rows", ("wa_raw1", "wa_raw0", "wa_grouped0", "wb_grouped1"))
+        d_rows = planes("d_rows", ("wa_raw0", "wa_raw1", "wa_grouped0", "w1_scales"))
         y_rows, sg, gated = planes("y_rows"), planes("sg"), planes("gated")
         z = [keep.tile([P, PACK, HALF], F32, name="z%d" % u) for u in range(2)]
 

@@ -132,9 +132,7 @@ def tile_picked_twtgxblse_none_po_kernel(
             nc.vector.tensor_copy(target[:].rearrange("p (t m) -> p t m", t=PACK), source[:].rearrange("p (m t) -> p t m", t=PACK))
 
         def pick_words(target, picks, name):
-            picked = keep.tile([P, S], U32, name=name, align_bytes=64)
-            nc.vector.tensor_copy(picked[:], x_codes[:].indirect(picks[:]))
-            deal_words(target, picked)
+            nc.vector.tensor_copy(dealt(target[:]), x_codes[:].indirect(picks[:]))
 
         def pick_bytes(target, picks, name, tag=""):
             picked = keep.tile([P, S], U8, name=name, tag=tag, align_bytes=64)
@@ -213,33 +211,20 @@ def tile_picked_twtgxblse_none_po_kernel(
 
         ex, ex_again, sums, logs, minus_h = planes("ex"), planes("ex_again"), planes("sums"), planes("logs"), planes("minus_h")
         for u, cols in enumerate(halves):
-            for t in range(PACK):
-                nc.scalar.activation(ex[t][:, cols], h_banks[u][t][:], ACT.Exp)
-            for t in [1, 2, 3]:
-                nc.scalar.activation(ex_again[t][:, cols], h_banks[u][t][:], ACT.Exp)
-        for u, t in [(0, t) for t in range(PACK)]:
-            nc.vector.tensor_scalar(minus_h[t][:, halves[u]], h_banks[u][t][:], -1.0, None, ALU.mult)
-        copied = [t for t in range(PACK) if t not in [1, 2, 3] and t not in []]
-        for t in copied[:1]:
-            nc.vector.tensor_copy(ex_again[t][:], ex[t][:])
-        for t in []:
-            for cols in halves:
-                nc.scalar.activation(ex_again[t][:, cols], ex[t][:].indirect(entries(n3_list, cols)), ACT.Copy)
+            for copies in (ex, ex_again):
+                for t in range(PACK):
+                    nc.scalar.activation(copies[t][:, cols], h_banks[u][t][:], ACT.Exp)
         for t in range(PACK):
-            if t + 1 in copied[1:]:
-                nc.vector.tensor_copy(ex_again[t + 1][:], ex[t + 1][:])
-            if t in []:
-                if t not in []:
-                    for cols in halves:
-                        nc.scalar.activation(ex_again[t][:, cols], ex[t][:].indirect(entries(n3_list, cols)), ACT.Copy)
-                nc.vector.tensor_tensor(sums[t][:], ex[t][:], ex_again[t][:], ALU.add)
-            else:
-                for cols in halves:
-                    nc.vector.tensor_tensor(sums[t][:, cols], ex[t][:].indirect(entries(n3_list, cols)), ex_again[t][:, cols], ALU.add)
-            nc.scalar.activation(logs[t][:], sums[t][:], ACT.Ln)
-            for u, cols in enumerate(halves):
-                if (u, t) not in [(0, t) for t in range(PACK)]:
-                    nc.scalar.activation(minus_h[t][:, cols], h_banks[u][t][:], ACT.Copy, scale=-1.0)
+            nc.vector.tensor_scalar(minus_h[t][:, halves[0]], h_banks[0][t][:], -1.0, None, ALU.mult)
+        for cols in halves:
+            for t in range(PACK):
+                nc.vector.tensor_tensor(sums[t][:, cols], ex[t][:].indirect(entries(n3_list, cols)), ex_again[t][:, cols], ALU.add)
+        for t in range(PACK):
+            nc.scalar.activation(logs[t][:, halves[0]], sums[t][:, halves[0]], ACT.Ln)
+        for t in range(PACK):
+            nc.scalar.activation(minus_h[t][:, halves[1]], h_banks[1][t][:], ACT.Copy, scale=-1.0)
+        for t in range(PACK):
+            nc.scalar.activation(logs[t][:, halves[1]], sums[t][:, halves[1]], ACT.Ln)
 
         out_q = mx_tiles("out_q", H)
         out_rows = out_0.rearrange("(p t) c -> p t c", t=PACK)

@@ -2,7 +2,7 @@ from contextlib import ExitStack
 
 import concourse.mybir as mybir
 
-K, T, S, N, H = 512, 2048, 512, 512, 512
+T, S, N, H = 2048, 512, 512, 512
 FLOPS = 3 * 2 * 512 * 512 * 512
 
 F32 = mybir.dt.float32
@@ -19,6 +19,13 @@ P = 128
 PACK = 4
 HALF = 256
 LIST_ROWS = 16
+QUADRANTS = 4
+LINE_WORDS = 4
+
+Y_TILES_ON_VECTOR = 2
+EX_COPIES_ON_VECTOR = 1
+FUSED_IN_LAST_HALF = 1
+FIRST_HALF_STEP = PACK + 2
 
 
 def tile_picked_twtgxblse_none_po_kernel(
@@ -26,71 +33,83 @@ def tile_picked_twtgxblse_none_po_kernel(
 ):
     nc = tc.nc
     halves = [slice(u * HALF, (u + 1) * HALF) for u in range(2)]
+    all_columns = slice(0, H)
 
     with ExitStack() as ctx:
         keep = ctx.enter_context(tc.tile_pool(name="keep", bufs=1))
         psum = ctx.enter_context(tc.psum_pool(name="psum", bufs=1))
-
-        def load_list(name, source):
-            tile = keep.tile([P, 512 // LIST_ROWS], U16, name=name)
-            nc.sync.dma_start(tile[:], source)
-            return tile
-
-        def entries(tile, cols):
-            return tile[:, cols.start // LIST_ROWS : cols.stop // LIST_ROWS]
-
-        def load_scale_rows(queue, tile, source):
-            for q in range(4):
-                queue.dma_start(tile[32 * q : 32 * q + 4, :].bitcast(I32), source[0, 4 * q : 4 * q + 4, :].bitcast(I32))
-
-        def load_words(tile, source):
-            nc.sync.dma_start(tile[:].bitcast(I32), source[0].rearrange("p c t -> p (c t)").bitcast(I32))
-
-        def load_weight_half(name, w, cols):
-            raw = keep.tile([P, PACK, HALF], F32, name=name, align_bytes=64)
-            nc.sync.dma_start(raw[:], w.rearrange("(p j) c -> p j c", j=PACK)[:, :, cols])
-            return raw
-
-        def load_rows(name, source):
-            tile = keep.tile([P, PACK], F32, name=name)
-            nc.scalar.dma_start(tile[:], source.rearrange("(p t) o -> p (t o)", t=PACK))
-            return tile
-
-        def interleave(copy, name, planes):
-            grouped = keep.tile([P, planes.shape[2], PACK], BF16, name=name, align_bytes=64)
-            copy(
-                grouped[:].rearrange("p (c i) t -> p c t i", i=4),
-                planes.rearrange("p t (c i) -> p c t i", i=4),
-            )
-            return grouped
-
-        def quantise(codes, scales, cols, grouped):
-            nc.vector.quantize_mx(
-                out=codes[:, cols].bitcast(FP8X4), scales=scales[:, cols], in_=grouped[:].rearrange("p c t -> p (c t)")
-            )
 
         def mx_tiles(name, width, codes_tag="", scales_tag=""):
             codes = keep.tile([P, width], U32, name=name + "_codes", tag=codes_tag, align_bytes=64)
             scales = keep.tile([P, width], U8, name=name + "_scales", tag=scales_tag, align_bytes=64)
             return codes, scales
 
-        def dealt(ap):
-            return ap.rearrange("p (t m) -> p m t", t=PACK)
+        def row_tiles(name, tags=("",) * PACK):
+            return [keep.tile([P, H], F32, name="%s%d" % (name, t), tag=tags[t], align_bytes=64) for t in range(PACK)]
 
-        def product(target, cols, lhs, t, rhs):
-            rows = slice(P * t, P * (t + 1))
+        def load_list(name, source):
+            tile = keep.tile([P, S // LIST_ROWS], U16, name=name)
+            nc.sync.dma_start(tile[:], source)
+            return tile
+
+        def load_words(tile, source):
+            nc.sync.dma_start(tile[:].bitcast(I32), source[0].rearrange("p c t -> p (c t)").bitcast(I32))
+
+        def load_scale_rows(tile, source):
+            for q in range(QUADRANTS):
+                nc.sync.dma_start(tile[32 * q : 32 * q + 4, :].bitcast(I32), source[0, 4 * q : 4 * q + 4, :].bitcast(I32))
+
+        def load_weight_half(name, w, cols):
+            raw = keep.tile([P, PACK, HALF], F32, name=name, align_bytes=64)
+            nc.sync.dma_start(raw[:], w.rearrange("(p j) c -> p j c", j=PACK)[:, :, cols])
+            return raw
+
+        def load_row_values(name, source):
+            tile = keep.tile([P, PACK], F32, name=name)
+            nc.scalar.dma_start(tile[:], source.rearrange("(p t) o -> p (t o)", t=PACK))
+            return tile
+
+        def entries(list_tile, cols):
+            return list_tile[:, cols.start // LIST_ROWS : cols.stop // LIST_ROWS]
+
+        def pick(name, dtype, table, list_tile, tag=""):
+            picked = keep.tile([P, S], dtype, name=name, tag=tag, align_bytes=64)
+            nc.vector.tensor_copy(picked[:], table[:].indirect(list_tile[:]))
+            return picked
+
+        def deal_words(target, source):
+            nc.vector.tensor_copy(
+                target[:].rearrange("p (t b i) -> p b t i", t=PACK, i=LINE_WORDS),
+                source[:].rearrange("p (b i t) -> p b t i", t=PACK, i=LINE_WORDS),
+            )
+
+        def deal_bytes(target, source):
+            nc.vector.tensor_copy(target[:].rearrange("p (t m) -> p t m", t=PACK), source[:].rearrange("p (m t) -> p t m", t=PACK))
+
+        def interleave(copy, name, source):
+            grouped = keep.tile([P, HALF, PACK], BF16, name=name, align_bytes=64)
+            copy(
+                grouped[:].rearrange("p (c i) t -> p c t i", i=LINE_WORDS),
+                source[:].rearrange("p t (c i) -> p c t i", i=LINE_WORDS),
+            )
+            return grouped
+
+        def quantise(target, cols, grouped):
+            nc.vector.quantize_mx(
+                out=target[0][:, cols].bitcast(FP8X4), scales=target[1][:, cols], in_=grouped[:].rearrange("p c t -> p (c t)")
+            )
+
+        def product(bank, stationary, t, moving, cols):
+            places = slice(P * t, P * (t + 1))
             nc.tensor.matmul_mx(
-                out=target,
-                lhsT=lhs[0][:, rows].bitcast(FP8X4),
-                lhsT_scale=lhs[1][:, rows],
-                rhs=rhs[0][:, cols].bitcast(FP8X4),
-                rhs_scale=rhs[1][:, cols],
+                out=bank[:],
+                lhsT=stationary[0][:, places].bitcast(FP8X4),
+                lhsT_scale=stationary[1][:, places],
+                rhs=moving[0][:, cols].bitcast(FP8X4),
+                rhs_scale=moving[1][:, cols],
                 start=True,
                 stop=True,
             )
-
-        def planes(name, tags=("",) * PACK):
-            return [keep.tile([P, H], F32, name="%s%d" % (name, t), tag=tags[t], align_bytes=64) for t in range(PACK)]
 
         x_codes, x_bytes = mx_tiles("x", T)
         w1_codes, w1_bytes = mx_tiles("w1", N)
@@ -99,19 +118,20 @@ def tile_picked_twtgxblse_none_po_kernel(
         two_list = load_list("two_list", two)
         offs_list = load_list("offs_list", offs)
         n1_list = load_list("n1_list", n1)
-        slope = load_rows("slope", sl)
-        threshold = load_rows("threshold", th)
-        gate = load_rows("gate", gt)
+        slope = load_row_values("slope", sl)
+        threshold = load_row_values("threshold", th)
+        gate = load_row_values("gate", gt)
         load_words(x_codes, x_words)
         wb_raw = [load_weight_half("wb_raw0", wb, halves[0])]
-        load_scale_rows(nc.sync, x_bytes, x_scales)
+        load_scale_rows(x_bytes, x_scales)
         n2_list = load_list("n2_list", n2)
         wb_raw.append(load_weight_half("wb_raw1", wb, halves[1]))
         wa_raw = [load_weight_half("wa_raw%d" % u, wa, halves[u]) for u in range(2)]
         load_words(w1_codes, w1_words)
-        load_scale_rows(nc.sync, w1_bytes, w1_scales)
+        load_scale_rows(w1_bytes, w1_scales)
         n3_list = load_list("n3_list", n3)
         n4_list = load_list("n4_list", n4)
+
         warm = keep.tile([P, 2], F32, name="warm")
         nc.vector.memset(warm[:, 0:1], 0.0)
         nc.scalar.activation(warm[:, 1:2], warm[:, 0:1], ACT.Sigmoid)
@@ -123,49 +143,38 @@ def tile_picked_twtgxblse_none_po_kernel(
         half_gate = keep.tile([P, PACK], F32, name="half_gate")
         nc.gpsimd.tensor_scalar(half_gate[:], gate[:], -0.5, 0.0, ALU.mult, ALU.add)
 
-        def deal_words(target, source):
-            nc.vector.tensor_copy(
-                target[:].rearrange("p (t b i) -> p b t i", t=PACK, i=4), source[:].rearrange("p (b i t) -> p b t i", t=PACK, i=4)
-            )
-
-        def deal_bytes(target, source):
-            nc.vector.tensor_copy(target[:].rearrange("p (t m) -> p t m", t=PACK), source[:].rearrange("p (m t) -> p t m", t=PACK))
-
-        def pick_words(target, picks, name):
-            nc.vector.tensor_copy(dealt(target[:]), x_codes[:].indirect(picks[:]))
-
-        def pick_bytes(target, picks, name, tag=""):
-            picked = keep.tile([P, S], U8, name=name, tag=tag, align_bytes=64)
-            nc.vector.tensor_copy(picked[:], x_bytes[:].indirect(picks[:]))
-            deal_bytes(target, picked)
-
-        banks = [psum.tile([P, H], F32, name="bank%d" % b) for b in range(2 * PACK)]
-        d_banks, y_banks = banks[:PACK], banks[PACK:]
-        wb_grouped = [interleave(nc.scalar.copy, "wb_grouped%d" % u, wb_raw[u][:]) for u in range(2)]
-        wa_grouped = [interleave(nc.scalar.copy, "wa_grouped%d" % u, wa_raw[u][:]) for u in range(2)]
-        x_two, x_idx, wb_q, wa_q = mx_tiles("x_two", S), mx_tiles("x_idx", S), mx_tiles("wb_q", H), mx_tiles("wa_q", H)
-        pick_words(x_two[0], two_list, "two_words")
-        pick_words(x_idx[0], offs_list, "offs_words")
-        pick_bytes(x_two[1], two_list, "two_bytes")
-        for u in range(2):
-            quantise(wb_q[0], wb_q[1], halves[u], wb_grouped[u])
-        pick_bytes(x_idx[1], offs_list, "offs_bytes", "wb_grouped1")
+        d_banks = [psum.tile([P, H], F32, name="bank%d" % t) for t in range(PACK)]
+        y_banks = [psum.tile([P, H], F32, name="bank%d" % (PACK + t)) for t in range(PACK)]
+        wb_grouped = [interleave(nc.scalar.copy, "wb_grouped%d" % u, wb_raw[u]) for u in range(2)]
+        wa_grouped = [interleave(nc.scalar.copy, "wa_grouped%d" % u, wa_raw[u]) for u in range(2)]
+        x_two, wb_q, wa_q = mx_tiles("x_two", S), mx_tiles("wb_q", H), mx_tiles("wa_q", H)
+        two_words = pick("two_words", U32, x_codes, two_list)
+        offs_words = pick("offs_words", U32, x_codes, offs_list)
+        deal_words(x_two[0], two_words)
+        two_bytes = pick("two_bytes", U8, x_bytes, two_list)
+        quantise(wb_q, halves[0], wb_grouped[0])
+        deal_bytes(x_two[1], two_bytes)
+        quantise(wb_q, halves[1], wb_grouped[1])
+        x_idx = mx_tiles("x_idx", S, codes_tag="wb_grouped1")
+        offs_bytes = pick("offs_bytes", U8, x_bytes, offs_list, tag="wb_raw1")
+        deal_words(x_idx[0], offs_words)
+        deal_bytes(x_idx[1], offs_bytes)
         for t in range(PACK):
-            product(d_banks[t][:], slice(0, H), x_two, t, wb_q)
+            product(d_banks[t], x_two, t, wb_q, all_columns)
         for u in range(2):
-            quantise(wa_q[0], wa_q[1], halves[u], wa_grouped[u])
+            quantise(wa_q, halves[u], wa_grouped[u])
         for t in range(PACK):
-            product(y_banks[t][:], slice(0, H), x_idx, t, wa_q)
+            product(y_banks[t], x_idx, t, wa_q, all_columns)
 
-        w1_dealt = mx_tiles("w1_dealt", N, "wa_grouped1", "w1_codes")
+        w1_dealt = mx_tiles("w1_dealt", N, codes_tag="wa_grouped1", scales_tag="w1_codes")
         deal_words(w1_dealt[0], w1_codes)
         deal_bytes(w1_dealt[1], w1_bytes)
 
-        d_rows = planes("d_rows", ("wa_raw0", "wa_raw1", "wa_grouped0", "w1_scales"))
-        y_rows, sg, gated = planes("y_rows"), planes("sg"), planes("gated")
+        d_rows = row_tiles("d_rows", ("wa_raw0", "wa_raw1", "wa_grouped0", "w1_scales"))
+        y_rows, sg, gated = row_tiles("y_rows"), row_tiles("sg"), row_tiles("gated")
         z = [keep.tile([P, PACK, HALF], F32, name="z%d" % u) for u in range(2)]
 
-        def gate_values(t, cols):
+        def fetch_sigmoid(t, cols):
             nc.scalar.activation(
                 sg[t][:, cols],
                 d_rows[t][:].indirect(entries(n1_list, cols)),
@@ -185,72 +194,68 @@ def tile_picked_twtgxblse_none_po_kernel(
         for t in range(PACK):
             nc.scalar.copy(d_rows[t][:], d_banks[t][:])
             if t > 0:
-                gate_values(t - 1, halves[0])
-        gate_values(PACK - 1, halves[0])
-        for t in range(3):
+                fetch_sigmoid(t - 1, halves[0])
+        fetch_sigmoid(PACK - 1, halves[0])
+        for t in range(Y_TILES_ON_VECTOR):
             nc.vector.tensor_scalar(y_rows[t][:], y_banks[t][:], half_gate[:, t : t + 1], None, ALU.mult)
-        for t in range(3, PACK):
+        for t in range(Y_TILES_ON_VECTOR, PACK):
             nc.scalar.activation(y_rows[t][:], y_banks[t][:], ACT.Copy, scale=half_gate[:, t : t + 1])
         for t in range(PACK):
-            gate_values(t, halves[1])
+            fetch_sigmoid(t, halves[1])
 
         z_q = mx_tiles("z_q", H)
-        h_banks = [[psum.tile([P, HALF], F32, name="bank%d" % (PACK * u + t)) for t in range(PACK)] for u in range(2)]
         steps = [(t, u) for u in range(2) for t in range(PACK)]
         for i, (t, u) in enumerate(steps):
             apply_gate(t, u)
             if i > 0:
                 mix(*steps[i - 1])
-            if i == 6:
-                quantise(z_q[0], z_q[1], halves[0], interleave(nc.scalar.copy, "z_grouped0", z[0][:]))
+            if i == FIRST_HALF_STEP:
+                quantise(z_q, halves[0], interleave(nc.scalar.copy, "z_grouped0", z[0]))
         mix(*steps[-1])
-        quantise(z_q[0], z_q[1], halves[1], interleave(nc.vector.tensor_copy, "z_grouped1", z[1][:]))
-        for u in range(2):
-            for t in range(PACK):
-                product(h_banks[u][t][:], halves[u], w1_dealt, t, z_q)
+        quantise(z_q, halves[1], interleave(nc.vector.tensor_copy, "z_grouped1", z[1]))
 
-        ex, ex_again, sums, logs, minus_h = planes("ex"), planes("ex_again"), planes("sums"), planes("logs"), planes("minus_h")
+        h_banks = [[psum.tile([P, HALF], F32, name="bank%d" % (PACK * u + t)) for t in range(PACK)] for u in range(2)]
         for u, cols in enumerate(halves):
-            for copies in (ex, ex_again):
-                for t in range(PACK):
-                    nc.scalar.activation(copies[t][:, cols], h_banks[u][t][:], ACT.Exp)
+            for t in range(PACK):
+                product(h_banks[u][t], w1_dealt, t, z_q, cols)
+
+        ex, ex_again, sums, logs = row_tiles("ex"), row_tiles("ex_again"), row_tiles("sums"), row_tiles("logs")
+        minus_h = row_tiles("minus_h")
+        for u, cols in enumerate(halves):
+            for t in range(PACK):
+                nc.scalar.activation(ex[t][:, cols], h_banks[u][t][:], ACT.Exp)
+            for t in range(EX_COPIES_ON_VECTOR, PACK):
+                nc.scalar.activation(ex_again[t][:, cols], h_banks[u][t][:], ACT.Exp)
         for t in range(PACK):
             nc.vector.tensor_scalar(minus_h[t][:, halves[0]], h_banks[0][t][:], -1.0, None, ALU.mult)
-        for cols in halves:
-            for t in range(PACK):
+        for t in range(EX_COPIES_ON_VECTOR):
+            nc.vector.tensor_copy(ex_again[t][:], ex[t][:])
+        for t in range(PACK):
+            for cols in halves:
                 nc.vector.tensor_tensor(sums[t][:, cols], ex[t][:].indirect(entries(n3_list, cols)), ex_again[t][:, cols], ALU.add)
-        for t in range(PACK):
-            nc.scalar.activation(logs[t][:, halves[0]], sums[t][:, halves[0]], ACT.Ln)
-        for t in range(PACK):
+            nc.scalar.activation(logs[t][:], sums[t][:], ACT.Ln)
             nc.scalar.activation(minus_h[t][:, halves[1]], h_banks[1][t][:], ACT.Copy, scale=-1.0)
-        for t in range(PACK):
-            nc.scalar.activation(logs[t][:, halves[1]], sums[t][:, halves[1]], ACT.Ln)
 
         out_q = mx_tiles("out_q", H)
         out_rows = out_0.rearrange("(p t) c -> p t c", t=PACK)
         out_words = out_1[0].rearrange("p c t -> p (c t)").bitcast(I32)
-        chunks = halves
         fetched = {}
-        for c, cols in enumerate(chunks):
+        for t in range(FUSED_IN_LAST_HALF, PACK):
+            fetched[1, t] = keep.tile([P, HALF], F32, name="fetched%d" % t)
+            nc.scalar.activation(fetched[1, t][:], minus_h[t][:].indirect(entries(n4_list, halves[1])), ACT.Copy)
+        out_grouped = []
+        for u, cols in enumerate(halves):
+            result = keep.tile([P, PACK, HALF], F32, name="result%d" % u)
             for t in range(PACK):
-                if (c, t) in [(1, 1), (1, 2), (1, 3)]:
-                    fetched[c, t] = keep.tile([P, cols.stop - cols.start], F32, name="fetched%d_%d" % (c, t))
-                    nc.scalar.activation(fetched[c, t][:], minus_h[t][:].indirect(entries(n4_list, cols)), ACT.Copy)
-        late = []
-        for c, cols in enumerate(chunks):
-            result = keep.tile([P, PACK, cols.stop - cols.start], F32, name="result%d" % c)
-            for t in range(PACK):
-                if (c, t) in fetched:
-                    nc.vector.tensor_tensor(result[:, t, :], fetched[c, t][:], logs[t][:, cols], ALU.add)
-                else:
-                    nc.vector.tensor_tensor(result[:, t, :], minus_h[t][:].indirect(entries(n4_list, cols)), logs[t][:, cols], ALU.add)
+                looked_up = fetched[u, t][:] if (u, t) in fetched else minus_h[t][:].indirect(entries(n4_list, cols))
+                nc.vector.tensor_tensor(result[:, t, :], looked_up, logs[t][:, cols], ALU.add)
                 if t % 2:
                     nc.sync.dma_start(out_rows[:, t - 1 : t + 1, cols], result[:, t - 1 : t + 1, :])
-            copy = nc.scalar.copy if c + 1 < len(chunks) else nc.vector.tensor_copy
-            late.append((cols, interleave(copy, "out_grouped%d" % c, result[:])))
-        for cols, grouped in late:
-            quantise(out_q[0], out_q[1], cols, grouped)
+            copy = nc.scalar.copy if u == 0 else nc.vector.tensor_copy
+            out_grouped.append(interleave(copy, "out_grouped%d" % u, result))
+        for u, cols in enumerate(halves):
+            quantise(out_q, cols, out_grouped[u])
             nc.sync.dma_start(out_words[:, cols], out_q[0][:, cols].bitcast(I32))
-        for q in range(4):
+        for q in range(QUADRANTS):
             queue = nc.scalar if q % 2 else nc.sync
             queue.dma_start(out_2[0, 4 * q : 4 * q + 4, :].bitcast(I32), out_q[1][32 * q : 32 * q + 4, :].bitcast(I32))

from contextlib import ExitStack

import concourse.mybir as mybir

T, S, N, H = 2048, 512, 512, 512
FLOPS = 3 * 2 * 512 * 512 * 512

F32 = mybir.dt.float32
BF16 = mybir.dt.bfloat16
I32 = mybir.dt.int32
U32 = mybir.dt.uint32
U16 = mybir.dt.uint16
U8 = mybir.dt.uint8
FP8X4 = mybir.dt.float8_e4m3fn_x4
ALU = mybir.AluOpType
ACT = mybir.ActivationFunctionType

P = 128
PACK = 4
HALF = 256
LIST_ROWS = 16
QUADRANTS = 4
LINE_WORDS = 4

Y_TILES_ON_VECTOR = 2
EX_COPIES_ON_VECTOR = 1
FUSED_IN_LAST_HALF = 1
FIRST_HALF_STEP = PACK + 2


def tile_picked_twtgxblse_none_po_kernel(
    tc, x_words, x_scales, wa, wb, sl, th, gt, w1_words, w1_scales, offs, two, n1, n2, n3, n4, out_0, out_1, out_2
):
    nc = tc.nc
    halves = [slice(u * HALF, (u + 1) * HALF) for u in range(2)]
    all_columns = slice(0, H)

    with ExitStack() as ctx:
        keep = ctx.enter_context(tc.tile_pool(name="keep", bufs=1))
        psum = ctx.enter_context(tc.psum_pool(name="psum", bufs=1))

        def mx_tiles(name, width, codes_tag="", scales_tag=""):
            codes = keep.tile([P, width], U32, name=name + "_codes", tag=codes_tag, align_bytes=64)
            scales = keep.tile([P, width], U8, name=name + "_scales", tag=scales_tag, align_bytes=64)
            return codes, scales

        def row_tiles(name, tags=("",) * PACK):
            return [keep.tile([P, H], F32, name="%s%d" % (name, t), tag=tags[t], align_bytes=64) for t in range(PACK)]

        def load_list(name, source):
            tile = keep.tile([P, S // LIST_ROWS], U16, name=name)
            nc.sync.dma_start(tile[:], source)
            return tile

        def load_words(tile, source):
            nc.sync.dma_start(tile[:].bitcast(I32), source[0].rearrange("p c t -> p (c t)").bitcast(I32))

        def load_scale_rows(tile, source):
            for q in range(QUADRANTS):
                nc.sync.dma_start(tile[32 * q : 32 * q + 4, :].bitcast(I32), source[0, 4 * q : 4 * q + 4, :].bitcast(I32))

        def load_weight_half(name, w, cols):
            raw = keep.tile([P, PACK, HALF], F32, name=name, align_bytes=64)
            nc.sync.dma_start(raw[:], w.rearrange("(p j) c -> p j c", j=PACK)[:, :, cols])
            return raw

        def load_row_values(name, source):
            tile = keep.tile([P, PACK], F32, name=name)
            nc.scalar.dma_start(tile[:], source.rearrange("(p t) o -> p (t o)", t=PACK))
            return tile

        def entries(list_tile, cols):
            return list_tile[:, cols.start // LIST_ROWS : cols.stop // LIST_ROWS]

        def pick(name, dtype, table, list_tile, tag=""):
            picked = keep.tile([P, S], dtype, name=name, tag=tag, align_bytes=64)
            nc.vector.tensor_copy(picked[:], table[:].indirect(list_tile[:]))
            return picked

        def deal_words(target, source):
            nc.vector.tensor_copy(
                target[:].rearrange("p (t b i) -> p b t i", t=PACK, i=LINE_WORDS),
                source[:].rearrange("p (b i t) -> p b t i", t=PACK, i=LINE_WORDS),
            )

        def deal_bytes(target, source):
            nc.vector.tensor_copy(target[:].rearrange("p (t m) -> p t m", t=PACK), source[:].rearrange("p (m t) -> p t m", t=PACK))

        def interleave(copy, name, source):
            grouped = keep.tile([P, HALF, PACK], BF16, name=name, align_bytes=64)
            copy(
                grouped[:].rearrange("p (c i) t -> p c t i", i=LINE_WORDS),
                source[:].rearrange("p t (c i) -> p c t i", i=LINE_WORDS),
            )
            return grouped

        def quantise(target, cols, grouped):
            nc.vector.quantize_mx(
                out=target[0][:, cols].bitcast(FP8X4), scales=target[1][:, cols], in_=grouped[:].rearrange("p c t -> p (c t)")
            )

        def product(bank, stationary, t, moving, cols):
            places = slice(P * t, P * (t + 1))
            nc.tensor.matmul_mx(
                out=bank[:],
                lhsT=stationary[0][:, places].bitcast(FP8X4),
                lhsT_scale=stationary[1][:, places],
                rhs=moving[0][:, cols].bitcast(FP8X4),
                rhs_scale=moving[1][:, cols],
                start=True,
                stop=True,
            )

        x_codes, x_bytes = mx_tiles("x", T)
        w1_codes, w1_bytes = mx_tiles("w1", N)
        nc.vector.memset(x_bytes[:].bitcast(I32), 0)
        nc.vector.memset(w1_bytes[:].bitcast(I32), 0)
        two_list = load_list("two_list", two)
        offs_list = load_list("offs_list", offs)
        n1_list = load_list("n1_list", n1)
        slope = load_row_values("slope", sl)
        threshold = load_row_values("threshold", th)
        gate = load_row_values("gate", gt)
        load_words(x_codes, x_words)
        wb_raw = [load_weight_half("wb_raw0", wb, halves[0])]
        load_scale_rows(x_bytes, x_scales)
        n2_list = load_list("n2_list", n2)
        wb_raw.append(load_weight_half("wb_raw1", wb, halves[1]))
        wa_raw = [load_weight_half("wa_raw%d" % u, wa, halves[u]) for u in range(2)]
        load_words(w1_codes, w1_words)
        load_scale_rows(w1_bytes, w1_scales)
        n3_list = load_list("n3_list", n3)
        n4_list = load_list("n4_list", n4)

        warm = keep.tile([P, 2], F32, name="warm")
        nc.vector.memset(warm[:, 0:1], 0.0)
        nc.scalar.activation(warm[:, 1:2], warm[:, 0:1], ACT.Sigmoid)

        slope_threshold = keep.tile([P, PACK], F32, name="slope_threshold")
        nc.gpsimd.tensor_tensor(slope_threshold[:], threshold[:], slope[:], ALU.mult)
        bias = keep.tile([P, PACK], F32, name="bias")
        nc.gpsimd.tensor_scalar(bias[:], slope_threshold[:], -1.0, 0.0, ALU.mult, ALU.add)
        half_gate = keep.tile([P, PACK], F32, name="half_gate")
        nc.gpsimd.tensor_scalar(half_gate[:], gate[:], -0.5, 0.0, ALU.mult, ALU.add)

        d_banks = [psum.tile([P, H], F32, name="bank%d" % t) for t in range(PACK)]
        y_banks = [psum.tile([P, H], F32, name="bank%d" % (PACK + t)) for t in range(PACK)]
        wb_grouped = [interleave(nc.scalar.copy, "wb_grouped%d" % u, wb_raw[u]) for u in range(2)]
        wa_grouped = [interleave(nc.scalar.copy, "wa_grouped%d" % u, wa_raw[u]) for u in range(2)]
        x_two, wb_q, wa_q = mx_tiles("x_two", S), mx_tiles("wb_q", H), mx_tiles("wa_q", H)
        two_words = pick("two_words", U32, x_codes, two_list)
        offs_words = pick("offs_words", U32, x_codes, offs_list)
        deal_words(x_two[0], two_words)
        two_bytes = pick("two_bytes", U8, x_bytes, two_list)
        quantise(wb_q, halves[0], wb_grouped[0])
        deal_bytes(x_two[1], two_bytes)
        quantise(wb_q, halves[1], wb_grouped[1])
        x_idx = mx_tiles("x_idx", S, codes_tag="wb_grouped1")
        offs_bytes = pick("offs_bytes", U8, x_bytes, offs_list, tag="wb_raw1")
        deal_words(x_idx[0], offs_words)
        deal_bytes(x_idx[1], offs_bytes)
        for t in range(PACK):
            product(d_banks[t], x_two, t, wb_q, all_columns)
        for u in range(2):
            quantise(wa_q, halves[u], wa_grouped[u])
        for t in range(PACK):
            product(y_banks[t], x_idx, t, wa_q, all_columns)

        w1_dealt = mx_tiles("w1_dealt", N, codes_tag="wa_grouped1", scales_tag="w1_codes")
        deal_words(w1_dealt[0], w1_codes)
        deal_bytes(w1_dealt[1], w1_bytes)

        d_rows = row_tiles("d_rows", ("wa_raw0", "wa_raw1", "wa_grouped0", "w1_scales"))
        y_rows, sg, gated = row_tiles("y_rows"), row_tiles("sg"), row_tiles("gated")
        z = [keep.tile([P, PACK, HALF], F32, name="z%d" % u) for u in range(2)]

        def fetch_sigmoid(t, cols):
            nc.scalar.activation(
                sg[t][:, cols],
                d_rows[t][:].indirect(entries(n1_list, cols)),
                ACT.Sigmoid,
                bias=bias[:, t : t + 1],
                scale=slope[:, t : t + 1],
            )

        def apply_gate(t, u):
            cols = halves[u]
            nc.vector.scalar_tensor_tensor(gated[t][:, cols], y_rows[t][:, cols], -2.0, sg[t][:, cols], ALU.mult, ALU.mult)

        def mix(t, u):
            cols = halves[u]
            nc.vector.tensor_tensor(z[u][:, t, :], y_rows[t][:].indirect(entries(n2_list, cols)), gated[t][:, cols], ALU.add)

        for t in range(PACK):
            nc.scalar.copy(d_rows[t][:], d_banks[t][:])
            if t > 0:
                fetch_sigmoid(t - 1, halves[0])
        fetch_sigmoid(PACK - 1, halves[0])
        for t in range(Y_TILES_ON_VECTOR):
            nc.vector.tensor_scalar(y_rows[t][:], y_banks[t][:], half_gate[:, t : t + 1], None, ALU.mult)
        for t in range(Y_TILES_ON_VECTOR, PACK):
            nc.scalar.activation(y_rows[t][:], y_banks[t][:], ACT.Copy, scale=half_gate[:, t : t + 1])
        for t in range(PACK):
            fetch_sigmoid(t, halves[1])

        z_q = mx_tiles("z_q", H)
        steps = [(t, u) for u in range(2) for t in range(PACK)]
        for i, (t, u) in enumerate(steps):
            apply_gate(t, u)
            if i > 0:
                mix(*steps[i - 1])
            if i == FIRST_HALF_STEP:
                quantise(z_q, halves[0], interleave(nc.scalar.copy, "z_grouped0", z[0]))
        mix(*steps[-1])
        quantise(z_q, halves[1], interleave(nc.vector.tensor_copy, "z_grouped1", z[1]))

        h_banks = [[psum.tile([P, HALF], F32, name="bank%d" % (PACK * u + t)) for t in range(PACK)] for u in range(2)]
        for u, cols in enumerate(halves):
            for t in range(PACK):
                product(h_banks[u][t], w1_dealt, t, z_q, cols)

        ex, ex_again, sums, logs = row_tiles("ex"), row_tiles("ex_again"), row_tiles("sums"), row_tiles("logs")
        minus_h = row_tiles("minus_h")
        for u, cols in enumerate(halves):
            for t in range(PACK):
                nc.scalar.activation(ex[t][:, cols], h_banks[u][t][:], ACT.Exp)
            for t in range(EX_COPIES_ON_VECTOR, PACK):
                nc.scalar.activation(ex_again[t][:, cols], h_banks[u][t][:], ACT.Exp)
        for t in range(PACK):
            nc.vector.tensor_scalar(minus_h[t][:, halves[0]], h_banks[0][t][:], -1.0, None, ALU.mult)
        for t in range(EX_COPIES_ON_VECTOR):
            nc.vector.tensor_copy(ex_again[t][:], ex[t][:])
        for t in range(PACK):
            for cols in halves:
                nc.vector.tensor_tensor(sums[t][:, cols], ex[t][:].indirect(entries(n3_list, cols)), ex_again[t][:, cols], ALU.add)
            nc.scalar.activation(logs[t][:], sums[t][:], ACT.Ln)
            nc.scalar.activation(minus_h[t][:, halves[1]], h_banks[1][t][:], ACT.Copy, scale=-1.0)

        out_q = mx_tiles("out_q", H)
        out_rows = out_0.rearrange("(p t) c -> p t c", t=PACK)
        out_words = out_1[0].rearrange("p c t -> p (c t)").bitcast(I32)
        fetched = {}
        for t in range(FUSED_IN_LAST_HALF, PACK):
            fetched[1, t] = keep.tile([P, HALF], F32, name="fetched%d" % t)
            nc.scalar.activation(fetched[1, t][:], minus_h[t][:].indirect(entries(n4_list, halves[1])), ACT.Copy)
        out_grouped = []
        for u, cols in enumerate(halves):
            result = keep.tile([P, PACK, HALF], F32, name="result%d" % u)
            for t in range(PACK):
                looked_up = fetched[u, t][:] if (u, t) in fetched else minus_h[t][:].indirect(entries(n4_list, cols))
                nc.vector.tensor_tensor(result[:, t, :], looked_up, logs[t][:, cols], ALU.add)
                if t % 2:
                    nc.sync.dma_start(out_rows[:, t - 1 : t + 1, cols], result[:, t - 1 : t + 1, :])
            copy = nc.scalar.copy if u == 0 else nc.vector.tensor_copy
            out_grouped.append(interleave(copy, "out_grouped%d" % u, result))
        for u, cols in enumerate(halves):
            quantise(out_q, cols, out_grouped[u])
            nc.sync.dma_start(out_words[:, cols], out_q[0][:, cols].bitcast(I32))
        for q in range(QUADRANTS):
            queue = nc.scalar if q % 2 else nc.sync
            queue.dma_start(out_2[0, 4 * q : 4 * q + 4, :].bitcast(I32), out_q[1][32 * q : 32 * q + 4, :].bitcast(I32))
